import numpy as np
CORES = [9,17,57,81,121,137,145,185,209,249]
N = 10
W, TIMES = 128, 2
def setup_inputs(rng):
    return {"b": rng.standard_normal((N, 128, W), dtype=np.float32)}
def op(p):
    return 3.0 * p - (np.roll(p, 1, 1) + np.roll(p, -1, 1)) - 0.25 * (np.roll(p, 2, 1) + np.roll(p, -2, 1))
def reference(b):
    e = np.concatenate(list(b.astype(np.float64)), axis=1)
    x = np.zeros_like(e); p = e.copy(); ee = (e * e).sum(axis=1, keepdims=True)
    for _ in range(TIMES):
        q = op(p)
        al = ee / (p * q).sum(axis=1, keepdims=True)
        x = x + al * p; e = e - al * q
        en = (e * e).sum(axis=1, keepdims=True)
        p = e + (en / ee) * p; ee = en
    return {"y": np.stack([x[:, W * i:W * i + W] for i in range(N)]).astype(np.float32)}

@@ -1,0 +1,235 @@
+from concourse.bass import DstId, RemoteDMATransfer
+from concourse.mybir import AluOpType, ActivationFunctionType
+
+NSIM = 256
+NR = 10
+MW = 24
+QUOTA = [2, 2, 2, 1]
+
+SCRATCH = {
+    "bS": ("sbuf", [128, 136], "float32"),
+    "b25S": ("sbuf", [128, 136], "float32"),
+    "a2S": ("sbuf", [128, 132], "float32"),
+    "wS": ("sbuf", [128, 144], "float32"),
+    "p1S": ("sbuf", [128, 128], "float32"),
+    "p3S": ("sbuf", [128, 132], "float32"),
+    "hwmS": ("sbuf", [128, 8], "float32"),
+    "junk": ("sbuf", [128, 720], "float32"),
+    "land": ("sbuf", [128, NR + 1, MW], "float32"),
+    "rl": ("sbuf", [128, MW], "float32"),
+    "prod": ("sbuf", [128, 152], "float32"),
+    "sc": ("sbuf", [128, 32], "float32"),
+    "z1S": ("sbuf", [128, 128], "float32"),
+    "zS": ("sbuf", [128, 128], "float32"),
+    "yS": ("sbuf", [128, 128], "float32"),
+    "b25P": ("psum", [128, 512], "float32"),
+    "a1P": ("psum", [128, 512], "float32"),
+    "w25P": ("psum", [128, 512], "float32"),
+    "hwP": ("psum", [128, 512], "float32"),
+    "z2P": ("psum", [128, 512], "float32"),
+}
+SEMAPHORES = ["ld", "dv", "ac", "arr", "rarr", "loc", "st"]
+
+
+def _bits(m):
+    return bin(m).count("1")
+
+
+def _plan(rc, cores, topo):
+    others = [d for d in cores if d != rc]
+    cross = [d for d in others if not topo.may_write(rc, d)]
+    same = [d for d in others if topo.may_write(rc, d)]
+    port = [c for c in range(NSIM)
+            if c not in cores and topo.host(c) == topo.host(rc) and topo.chip(c) == topo.chip(rc)
+            and all(topo.may_write(c, d) for d in others)]
+    port.sort(key=lambda c: (topo.die(c) != topo.die(rc), c))
+    todo = cross + same
+    jobs, pos = [], 0
+    for h, n in zip(port, QUOTA):
+        jobs.append((h, todo[pos:pos + n]))
+        pos += n
+    return jobs, todo[pos:]
+
+
+def _send(g, T, topo, core, src_ap, src_rank, dests):
+    m = topo.mask(core, dests[0])
+    for d in dests:
+        m &= topo.mask(core, d)
+    ids, aps = [], []
+    for d in dests:
+        rid, pid = topo.addr(d, core)
+        ids.append(DstId(rid=rid, pnc=pid))
+        aps.append(T.land[:, (src_rank - T.rank_of(d)) % NR, :])
+    g.remote_dma_fused([RemoteDMATransfer(dst_ids=ids, dma_engine_mask=m, remote_sem=T.sem.arr,
+                                          srcs=[src_ap], dsts=aps, alu_op=0)], local_sem=T.sem.loc)
+    return _bits(m)
+
+
+def rank_program(g, core, T, topo):
+    cores = list(T.cores)
+    rank = T.rank_of(core)
+    if rank is None:
+        for rc in cores:
+            if topo.host(rc) != topo.host(core) or topo.chip(rc) != topo.chip(core):
+                continue
+            for h, dests in _plan(rc, cores, topo)[0]:
+                if h == core and dests:
+                    g.wait_ge(T.sem.rarr, _bits(topo.mask(rc, core)))
+                    n = _send(g, T, topo, core, T.rl[:], T.rank_of(rc), dests)
+                    g.wait_ge(T.sem.loc, n)
+        return
+
+    v, a = g.vector, g.scalar
+    AL, AF = AluOpType, ActivationFunctionType
+    bS, b25S, a2S, wS, p1S, p3S, hwmS = T.bS, T.b25S, T.a2S, T.wS, T.p1S, T.p3S, T.hwmS
+    junk, land, prod, sc = T.junk, T.land, T.prod, T.sc
+    b25P, a1P, w25P, hwP, z2P = T.b25P, T.a1P, T.w25P, T.hwP, T.z2P
+    cnt = {"dv": 0, "ac": 0}
+    seen = {}
+
+    def need(q, toks):
+        qn = {0: "v", 1: "a", 2: "g", 3: "s"}[q]
+        qq = (v, a, g, g.sync)[q]
+        for s, val in toks:
+            if seen.get((qn, s), 0) < val:
+                qq.wait_ge(T.sem[s], val)
+                seen[(qn, s)] = val
+
+    def V(inst):
+        inst.then_inc(T.sem.dv, 1)
+        cnt["dv"] += 1
+        return ("dv", cnt["dv"])
+
+    def A(inst):
+        inst.then_inc(T.sem.ac, 1)
+        cnt["ac"] += 1
+        return ("ac", cnt["ac"])
+
+    def msg(lo, hi):
+        return land[:, 0, lo:hi]
+
+    arr_total = 0
+    for rc in cores:
+        if rc == core:
+            continue
+        jobs, own = _plan(rc, cores, topo)
+        for snd, dests in jobs + [(rc, own)]:
+            if core in dests:
+                m = topo.mask(snd, dests[0])
+                for d in dests:
+                    m &= topo.mask(snd, d)
+                arr_total += _bits(m)
+    ARR = ("arr", arr_total)
+    LD = ("ld", 16)
+
+    g.sync.dma_start(bS[:, 4:132], T.b[:]).then_inc(T.sem.ld, 16)
+    V(v.memset(bS[:, 0:4], 0.0))
+    V(v.memset(bS[:, 132:136], 0.0))
+    V(v.memset(wS[:, 0:6], 0.0))
+    V(v.memset(wS[:, 138:144], 0.0))
+    V(v.memset(msg(12, 13), 0.5))
+    fills = V(v.memset(msg(17, 18), 0.5))
+
+    need(1, [LD, fills])
+    A(a.activation(b25P[:, 0:136], bS[:], AF.Copy, scale=0.25))
+    a2 = A(a.activation(b25S[:], bS[:], AF.Copy, scale=0.25))
+    a3 = A(a.activation(junk[:, 0:128], bS[:, 4:132], AF.Square, accum_out=sc[:, 0:1]))
+    A(a.activation(msg(2, 4), bS[:, 130:132], AF.Copy))
+    need(1, [a3])
+    A(a.activation(msg(0, 1), sc[:, 0:1], AF.Copy, scale=0.5))
+    need(0, [LD, fills])
+    V(v.tensor_tensor(a1P[:, 0:132], bS[:, 1:133], bS[:, 3:135], AL.add))
+    need(0, [a2])
+    v2 = V(v.tensor_tensor(a2S[:], b25P[:, 0:132], b25S[:, 4:136], AL.add))
+    need(0, [v2])
+    v3 = V(v.tensor_tensor(wS[:, 6:138], a1P[:, 0:132], a2S[:], AL.add))
+
+    need(1, [v3])
+    a5 = A(a.activation(w25P[:, 0:144], wS[:], AF.Copy, scale=0.25))
+    A(a.activation(msg(5, 11), wS[:, 132:138], AF.Copy))
+    A(a.activation(msg(13, 17), wS[:, 6:10], AF.Copy))
+    A(a.activation(junk[:, 144:276], wS[:, 6:138], AF.Square, accum_out=msg(11, 12)))
+    need(0, [v3])
+    v4 = V(v.tensor_tensor(p1S[:], bS[:, 4:132], wS[:, 8:136], AL.mult))
+    need(0, [a5])
+    v5 = V(v.tensor_tensor(hwP[:, 0:134], wS[:, 5:139], w25P[:, 6:140], AL.add))
+    need(0, [v5])
+    v6 = V(v.tensor_tensor(p3S[:], wS[:, 6:138], hwP[:, 2:134], AL.mult))
+    v7 = V(v.tensor_tensor(hwmS[:, 0:6], wS[:, 3:9], w25P[:, 2:8], AL.add))
+    need(0, [v7])
+    v8 = V(v.tensor_tensor(msg(18, 24), hwP[:, 0:6], hwmS[:, 0:6], AL.add))
+    need(1, [v4])
+    A(a.activation(junk[:, 288:416], p1S[:], AF.Copy, accum_out=msg(1, 2)))
+    need(1, [v6])
+    a10 = A(a.activation(junk[:, 432:564], p3S[:], AF.Copy, scale=2.0, accum_out=msg(4, 5)))
+
+    jobs, own = _plan(core, cores, topo)
+    jobs = [(h, d) for h, d in jobs if d]
+    need(2, [a10, v8])
+    hm = topo.mask(core, jobs[0][0])
+    ids = []
+    for h, _d in jobs:
+        hm &= topo.mask(core, h)
+        rid, pid = topo.addr(h, core)
+        ids.append(DstId(rid=rid, pnc=pid))
+    g.remote_dma_fused([RemoteDMATransfer(dst_ids=ids, dma_engine_mask=hm, remote_sem=T.sem.rarr,
+                                          srcs=[land[:, 0, :]], dsts=[T.rl[:] for _h in jobs], alu_op=0)],
+                       local_sem=T.sem.loc)
+    left = _bits(hm)
+    if own:
+        left += _send(g, T, topo, core, land[:, 0, :], rank, own)
+    need(1, [v8, a10])
+    a11 = A(a.activation(land[:, NR, 12:24], land[:, 0, 12:24], AF.Copy))
+
+    need(0, [ARR, a11])
+    g3 = V(v.tensor_tensor(prod[:, 80:150], land[:, 0:NR, 4:11], land[:, 1:NR + 1, 17:24], AL.mult))
+    g2 = V(v.tensor_tensor(prod[:, 30:80], land[:, 0:NR, 7:12], land[:, 1:NR + 1, 13:18], AL.mult))
+    g1 = V(v.tensor_tensor(prod[:, 0:30], land[:, 0:NR, 1:4], land[:, 1:NR + 1, 12:15], AL.mult))
+    V(v.tensor_tensor(wS[:, 8:10], wS[:, 8:10], land[:, NR - 1, 9:11], AL.add))
+    h2 = V(v.tensor_tensor(wS[:, 134:136], wS[:, 134:136], land[:, 1, 13:15], AL.add))
+    Nc, s1c = sc[:, 4:5], sc[:, 5:6]
+    need(1, [ARR, a11])
+    r0 = A(a.activation(junk[:, 576:586], land[:, 0:NR, 0], AF.Copy, accum_out=Nc))
+    need(1, [r0])
+    A(a.activation(sc[:, 8:9], Nc, AF.Copy, scale=3.0))
+    A(a.activation(sc[:, 10:11], Nc, AF.Square))
+    need(1, [g3])
+    A(a.activation(junk[:, 588:658], prod[:, 80:150], AF.Copy, accum_out=sc[:, 7:8]))
+    need(1, [g2])
+    A(a.activation(junk[:, 660:710], prod[:, 30:80], AF.Copy, accum_out=sc[:, 6:7]))
+    need(1, [g1])
+    r1 = A(a.activation(junk[:, 0:30], prod[:, 0:30], AF.Copy, accum_out=s1c))
+    need(1, [r1])
+    dd = A(a.activation(sc[:, 9:10], s1c, AF.Identity, bias=sc[:, 8:9], scale=-1.0))
+
+    Pc, Ec, njc = sc[:, 24:25], sc[:, 25:26], sc[:, 26:27]
+    need(0, [r1])
+    V(v.tensor_scalar(sc[:, 16:19], sc[:, 5:8], Nc, None, AL.mult))
+    t2 = V(v.tensor_scalar(sc[:, 20:22], sc[:, 5:7], s1c, None, AL.mult))
+    need(0, [t2])
+    t3 = V(v.tensor_tensor(sc[:, 25:27], sc[:, 17:19], sc[:, 20:22], AL.subtract))
+    need(0, [t3])
+    t4 = V(v.tensor_scalar(Pc, Ec, 3.0, njc, AL.mult, AL.subtract))
+    need(1, [t3])
+    A(a.activation(sc[:, 11:12], Ec, AF.Copy, scale=s1c))
+    e2 = A(a.activation(sc[:, 12:13], Ec, AF.Square))
+    need(1, [h2])
+    A(a.activation(z2P[:, 0:128], wS[:, 8:136], AF.Copy, scale=Ec))
+    need(1, [t4])
+    z1 = A(a.activation(T.z1S[:], bS[:, 4:132], AF.Copy, scale=Pc))
+    need(0, [t4, e2, dd])
+    t5 = V(v.tensor_scalar(sc[:, 13:14], Pc, Nc, sc[:, 11:12], AL.mult, AL.add))
+    need(0, [t5])
+    t6 = V(v.tensor_scalar(sc[:, 14:15], sc[:, 13:14], sc[:, 9:10], sc[:, 12:13], AL.mult, AL.subtract))
+    need(0, [t6])
+    V(v.reciprocal(sc[:, 15:16], sc[:, 14:15]))
+    need(0, [z1])
+    t8 = V(v.tensor_tensor(T.zS[:], T.z1S[:], z2P[:, 0:128], AL.add))
+    need(0, [t8])
+    t9 = V(v.tensor_scalar(T.yS[:], T.zS[:], sc[:, 15:16], sc[:, 10:11], AL.mult, AL.mult))
+
+    need(3, [t9])
+    g.sync.dma_start(T.y[:], T.yS[:]).then_inc(T.sem.st, 16)
+    g.sync.wait_ge(T.sem.st, 16)
+    g.wait_ge(T.sem.loc, left)
+    need(2, [("dv", cnt["dv"]), ("ac", cnt["ac"])])

@@ -4,6 +4,7 @@ from concourse.mybir import AluOpType, ActivationFunctionType
 NSIM = 256
 NR = 10
 MW = 24
+CUT = 22
 QUOTA = [2, 2, 2, 1]
 
 SCRATCH = {
@@ -28,11 +29,18 @@ SCRATCH = {
     "hwP": ("psum", [128, 512], "float32"),
     "z2P": ("psum", [128, 512], "float32"),
 }
-SEMAPHORES = ["ld", "dv", "ac", "arr", "rarr", "loc", "st"]
+SEMAPHORES = ["ld", "dv", "ac", "arr", "rarr1", "rarr2", "loc", "st"]
 
 
 def _bits(m):
     return bin(m).count("1")
+
+
+def _mask(topo, snd, dests):
+    m = topo.mask(snd, dests[0])
+    for d in dests:
+        m &= topo.mask(snd, d)
+    return m
 
 
 def _plan(rc, cores, topo):
@@ -46,22 +54,33 @@ def _plan(rc, cores, topo):
     todo = cross + same
     jobs, pos = [], 0
     for h, n in zip(port, QUOTA):
-        jobs.append((h, todo[pos:pos + n]))
+        if todo[pos:pos + n]:
+            jobs.append((h, todo[pos:pos + n]))
         pos += n
     return jobs, todo[pos:]
 
 
-def _send(g, T, topo, core, src_ap, src_rank, dests):
-    m = topo.mask(core, dests[0])
-    for d in dests:
-        m &= topo.mask(core, d)
+def _send(g, T, topo, core, src_ap, src_rank, dests, lo, hi):
+    m = _mask(topo, core, dests)
     ids, aps = [], []
     for d in dests:
         rid, pid = topo.addr(d, core)
         ids.append(DstId(rid=rid, pnc=pid))
-        aps.append(T.land[:, (src_rank - T.rank_of(d)) % NR, :])
+        aps.append(T.land[:, (src_rank - T.rank_of(d)) % NR, lo:hi])
     g.remote_dma_fused([RemoteDMATransfer(dst_ids=ids, dma_engine_mask=m, remote_sem=T.sem.arr,
                                           srcs=[src_ap], dsts=aps, alu_op=0)], local_sem=T.sem.loc)
+    return _bits(m)
+
+
+def _hand(g, T, topo, core, src_ap, helpers, lo, hi, sem):
+    m = _mask(topo, core, helpers)
+    ids = []
+    for h in helpers:
+        rid, pid = topo.addr(h, core)
+        ids.append(DstId(rid=rid, pnc=pid))
+    g.remote_dma_fused([RemoteDMATransfer(dst_ids=ids, dma_engine_mask=m, remote_sem=sem,
+                                          srcs=[src_ap], dsts=[T.rl[:, lo:hi] for _h in helpers], alu_op=0)],
+                       local_sem=T.sem.loc)
     return _bits(m)
 
 
@@ -72,10 +91,14 @@ def rank_program(g, core, T, topo):
         for rc in cores:
             if topo.host(rc) != topo.host(core) or topo.chip(rc) != topo.chip(core):
                 continue
-            for h, dests in _plan(rc, cores, topo)[0]:
-                if h == core and dests:
-                    g.wait_ge(T.sem.rarr, _bits(topo.mask(rc, core)))
-                    n = _send(g, T, topo, core, T.rl[:], T.rank_of(rc), dests)
+            jobs = _plan(rc, cores, topo)[0]
+            for h, dests in jobs:
+                if h == core:
+                    k = _bits(_mask(topo, rc, [x for x, _d in jobs]))
+                    g.wait_ge(T.sem.rarr1, k)
+                    n = _send(g, T, topo, core, T.rl[:, CUT:MW], T.rank_of(rc), dests, CUT, MW)
+                    g.wait_ge(T.sem.rarr2, k)
+                    n += _send(g, T, topo, core, T.rl[:, 0:CUT], T.rank_of(rc), dests, 0, CUT)
                     g.wait_ge(T.sem.loc, n)
         return
 
@@ -115,26 +138,29 @@ def rank_program(g, core, T, topo):
         jobs, own = _plan(rc, cores, topo)
         for snd, dests in jobs + [(rc, own)]:
             if core in dests:
-                m = topo.mask(snd, dests[0])
-                for d in dests:
-                    m &= topo.mask(snd, d)
-                arr_total += _bits(m)
+                arr_total += 2 * _bits(_mask(topo, snd, dests))
     ARR = ("arr", arr_total)
     LD = ("ld", 16)
+    jobs, own = _plan(core, cores, topo)
+    helpers = [h for h, _d in jobs]
 
     g.sync.dma_start(bS[:, 4:132], T.b[:]).then_inc(T.sem.ld, 16)
     V(v.memset(bS[:, 0:4], 0.0))
     V(v.memset(bS[:, 132:136], 0.0))
     V(v.memset(wS[:, 0:6], 0.0))
     V(v.memset(wS[:, 138:144], 0.0))
-    V(v.memset(msg(12, 13), 0.5))
-    fills = V(v.memset(msg(17, 18), 0.5))
+    V(v.memset(msg(9, 10), 0.5))
+    fills = V(v.memset(msg(14, 15), 0.5))
+
+    need(2, [LD])
+    left = _hand(g, T, topo, core, bS[:, 130:132], helpers, CUT, MW, T.sem.rarr1)
+    left += _send(g, T, topo, core, bS[:, 130:132], rank, own, CUT, MW)
 
     need(1, [LD, fills])
     A(a.activation(b25P[:, 0:136], bS[:], AF.Copy, scale=0.25))
     a2 = A(a.activation(b25S[:], bS[:], AF.Copy, scale=0.25))
     a3 = A(a.activation(junk[:, 0:128], bS[:, 4:132], AF.Square, accum_out=sc[:, 0:1]))
-    A(a.activation(msg(2, 4), bS[:, 130:132], AF.Copy))
+    A(a.activation(msg(22, 24), bS[:, 130:132], AF.Copy))
     need(1, [a3])
     A(a.activation(msg(0, 1), sc[:, 0:1], AF.Copy, scale=0.5))
     need(0, [LD, fills])
@@ -146,9 +172,9 @@ def rank_program(g, core, T, topo):
 
     need(1, [v3])
     a5 = A(a.activation(w25P[:, 0:144], wS[:], AF.Copy, scale=0.25))
-    A(a.activation(msg(5, 11), wS[:, 132:138], AF.Copy))
-    A(a.activation(msg(13, 17), wS[:, 6:10], AF.Copy))
-    A(a.activation(junk[:, 144:276], wS[:, 6:138], AF.Square, accum_out=msg(11, 12)))
+    A(a.activation(msg(2, 8), wS[:, 132:138], AF.Copy))
+    A(a.activation(msg(10, 14), wS[:, 6:10], AF.Copy))
+    A(a.activation(junk[:, 144:276], wS[:, 6:138], AF.Square, accum_out=msg(8, 9)))
     need(0, [v3])
     v4 = V(v.tensor_tensor(p1S[:], bS[:, 4:132], wS[:, 8:136], AL.mult))
     need(0, [a5])
@@ -157,36 +183,24 @@ def rank_program(g, core, T, topo):
     v6 = V(v.tensor_tensor(p3S[:], wS[:, 6:138], hwP[:, 2:134], AL.mult))
     v7 = V(v.tensor_tensor(hwmS[:, 0:6], wS[:, 3:9], w25P[:, 2:8], AL.add))
     need(0, [v7])
-    v8 = V(v.tensor_tensor(msg(18, 24), hwP[:, 0:6], hwmS[:, 0:6], AL.add))
+    v8 = V(v.tensor_tensor(msg(15, 21), hwP[:, 0:6], hwmS[:, 0:6], AL.add))
     need(1, [v4])
-    A(a.activation(junk[:, 288:416], p1S[:], AF.Copy, accum_out=msg(1, 2)))
+    A(a.activation(junk[:, 288:416], p1S[:], AF.Copy, accum_out=msg(21, 22)))
     need(1, [v6])
-    a10 = A(a.activation(junk[:, 432:564], p3S[:], AF.Copy, scale=2.0, accum_out=msg(4, 5)))
+    a10 = A(a.activation(junk[:, 432:564], p3S[:], AF.Copy, scale=2.0, accum_out=msg(1, 2)))
 
-    jobs, own = _plan(core, cores, topo)
-    jobs = [(h, d) for h, d in jobs if d]
     need(2, [a10, v8])
-    hm = topo.mask(core, jobs[0][0])
-    ids = []
-    for h, _d in jobs:
-        hm &= topo.mask(core, h)
-        rid, pid = topo.addr(h, core)
-        ids.append(DstId(rid=rid, pnc=pid))
-    g.remote_dma_fused([RemoteDMATransfer(dst_ids=ids, dma_engine_mask=hm, remote_sem=T.sem.rarr,
-                                          srcs=[land[:, 0, :]], dsts=[T.rl[:] for _h in jobs], alu_op=0)],
-                       local_sem=T.sem.loc)
-    left = _bits(hm)
-    if own:
-        left += _send(g, T, topo, core, land[:, 0, :], rank, own)
+    left += _hand(g, T, topo, core, msg(0, CUT), helpers, 0, CUT, T.sem.rarr2)
+    left += _send(g, T, topo, core, msg(0, CUT), rank, own, 0, CUT)
     need(1, [v8, a10])
-    a11 = A(a.activation(land[:, NR, 12:24], land[:, 0, 12:24], AF.Copy))
+    a11 = A(a.activation(land[:, NR, 9:21], land[:, 0, 9:21], AF.Copy))
 
     need(0, [ARR, a11])
-    g3 = V(v.tensor_tensor(prod[:, 80:150], land[:, 0:NR, 4:11], land[:, 1:NR + 1, 17:24], AL.mult))
-    g2 = V(v.tensor_tensor(prod[:, 30:80], land[:, 0:NR, 7:12], land[:, 1:NR + 1, 13:18], AL.mult))
-    g1 = V(v.tensor_tensor(prod[:, 0:30], land[:, 0:NR, 1:4], land[:, 1:NR + 1, 12:15], AL.mult))
-    V(v.tensor_tensor(wS[:, 8:10], wS[:, 8:10], land[:, NR - 1, 9:11], AL.add))
-    h2 = V(v.tensor_tensor(wS[:, 134:136], wS[:, 134:136], land[:, 1, 13:15], AL.add))
+    g3 = V(v.tensor_tensor(prod[:, 80:150], land[:, 0:NR, 1:8], land[:, 1:NR + 1, 14:21], AL.mult))
+    g2 = V(v.tensor_tensor(prod[:, 30:80], land[:, 0:NR, 4:9], land[:, 1:NR + 1, 10:15], AL.mult))
+    g1 = V(v.tensor_tensor(prod[:, 0:30], land[:, 0:NR, 21:24], land[:, 1:NR + 1, 9:12], AL.mult))
+    V(v.tensor_tensor(wS[:, 8:10], wS[:, 8:10], land[:, NR - 1, 6:8], AL.add))
+    h2 = V(v.tensor_tensor(wS[:, 134:136], wS[:, 134:136], land[:, 1, 10:12], AL.add))
     Nc, s1c = sc[:, 4:5], sc[:, 5:6]
     need(1, [ARR, a11])
     r0 = A(a.activation(junk[:, 576:586], land[:, 0:NR, 0], AF.Copy, accum_out=Nc))

from concourse.bass import DstId, RemoteDMATransfer
from concourse.mybir import AluOpType, ActivationFunctionType

NSIM = 256
NR = 10
MW = 24
CUT = 22
QUOTA = [2, 2, 2, 1]

SCRATCH = {
    "bS": ("sbuf", [128, 136], "float32"),
    "b25S": ("sbuf", [128, 136], "float32"),
    "a2S": ("sbuf", [128, 132], "float32"),
    "wS": ("sbuf", [128, 144], "float32"),
    "p1S": ("sbuf", [128, 128], "float32"),
    "p3S": ("sbuf", [128, 132], "float32"),
    "hwmS": ("sbuf", [128, 8], "float32"),
    "junk": ("sbuf", [128, 720], "float32"),
    "land": ("sbuf", [128, NR + 1, MW], "float32"),
    "rl": ("sbuf", [128, MW], "float32"),
    "prod": ("sbuf", [128, 152], "float32"),
    "sc": ("sbuf", [128, 32], "float32"),
    "z1S": ("sbuf", [128, 128], "float32"),
    "zS": ("sbuf", [128, 128], "float32"),
    "yS": ("sbuf", [128, 128], "float32"),
    "b25P": ("psum", [128, 512], "float32"),
    "a1P": ("psum", [128, 512], "float32"),
    "w25P": ("psum", [128, 512], "float32"),
    "hwP": ("psum", [128, 512], "float32"),
    "z2P": ("psum", [128, 512], "float32"),
}
SEMAPHORES = ["ld", "dv", "ac", "arr", "rarr1", "rarr2", "loc", "st"]


def _bits(m):
    return bin(m).count("1")


def _mask(topo, snd, dests):
    m = topo.mask(snd, dests[0])
    for d in dests:
        m &= topo.mask(snd, d)
    return m


def _plan(rc, cores, topo):
    others = [d for d in cores if d != rc]
    cross = [d for d in others if not topo.may_write(rc, d)]
    same = [d for d in others if topo.may_write(rc, d)]
    port = [c for c in range(NSIM)
            if c not in cores and topo.host(c) == topo.host(rc) and topo.chip(c) == topo.chip(rc)
            and all(topo.may_write(c, d) for d in others)]
    port.sort(key=lambda c: (topo.die(c) != topo.die(rc), c))
    todo = cross + same
    jobs, pos = [], 0
    for h, n in zip(port, QUOTA):
        if todo[pos:pos + n]:
            jobs.append((h, todo[pos:pos + n]))
        pos += n
    return jobs, todo[pos:]


def _send(g, T, topo, core, src_ap, src_rank, dests, lo, hi):
    m = _mask(topo, core, dests)
    ids, aps = [], []
    for d in dests:
        rid, pid = topo.addr(d, core)
        ids.append(DstId(rid=rid, pnc=pid))
        aps.append(T.land[:, (src_rank - T.rank_of(d)) % NR, lo:hi])
    g.remote_dma_fused([RemoteDMATransfer(dst_ids=ids, dma_engine_mask=m, remote_sem=T.sem.arr,
                                          srcs=[src_ap], dsts=aps, alu_op=0)], local_sem=T.sem.loc)
    return _bits(m)


def _hand(g, T, topo, core, src_ap, helpers, lo, hi, sem):
    m = _mask(topo, core, helpers)
    ids = []
    for h in helpers:
        rid, pid = topo.addr(h, core)
        ids.append(DstId(rid=rid, pnc=pid))
    g.remote_dma_fused([RemoteDMATransfer(dst_ids=ids, dma_engine_mask=m, remote_sem=sem,
                                          srcs=[src_ap], dsts=[T.rl[:, lo:hi] for _h in helpers], alu_op=0)],
                       local_sem=T.sem.loc)
    return _bits(m)


def rank_program(g, core, T, topo):
    cores = list(T.cores)
    rank = T.rank_of(core)
    if rank is None:
        for rc in cores:
            if topo.host(rc) != topo.host(core) or topo.chip(rc) != topo.chip(core):
                continue
            jobs = _plan(rc, cores, topo)[0]
            for h, dests in jobs:
                if h == core:
                    k = _bits(_mask(topo, rc, [x for x, _d in jobs]))
                    g.wait_ge(T.sem.rarr1, k)
                    n = _send(g, T, topo, core, T.rl[:, CUT:MW], T.rank_of(rc), dests, CUT, MW)
                    g.wait_ge(T.sem.rarr2, k)
                    n += _send(g, T, topo, core, T.rl[:, 0:CUT], T.rank_of(rc), dests, 0, CUT)
                    g.wait_ge(T.sem.loc, n)
        return

    v, a = g.vector, g.scalar
    AL, AF = AluOpType, ActivationFunctionType
    bS, b25S, a2S, wS, p1S, p3S, hwmS = T.bS, T.b25S, T.a2S, T.wS, T.p1S, T.p3S, T.hwmS
    junk, land, prod, sc = T.junk, T.land, T.prod, T.sc
    b25P, a1P, w25P, hwP, z2P = T.b25P, T.a1P, T.w25P, T.hwP, T.z2P
    cnt = {"dv": 0, "ac": 0}
    seen = {}

    def need(q, toks):
        qn = {0: "v", 1: "a", 2: "g", 3: "s"}[q]
        qq = (v, a, g, g.sync)[q]
        for s, val in toks:
            if seen.get((qn, s), 0) < val:
                qq.wait_ge(T.sem[s], val)
                seen[(qn, s)] = val

    def V(inst):
        inst.then_inc(T.sem.dv, 1)
        cnt["dv"] += 1
        return ("dv", cnt["dv"])

    def A(inst):
        inst.then_inc(T.sem.ac, 1)
        cnt["ac"] += 1
        return ("ac", cnt["ac"])

    def msg(lo, hi):
        return land[:, 0, lo:hi]

    arr_total = 0
    for rc in cores:
        if rc == core:
            continue
        jobs, own = _plan(rc, cores, topo)
        for snd, dests in jobs + [(rc, own)]:
            if core in dests:
                arr_total += 2 * _bits(_mask(topo, snd, dests))
    ARR = ("arr", arr_total)
    LD = ("ld", 16)
    jobs, own = _plan(core, cores, topo)
    helpers = [h for h, _d in jobs]

    g.sync.dma_start(bS[:, 4:132], T.b[:]).then_inc(T.sem.ld, 16)
    V(v.memset(bS[:, 0:4], 0.0))
    V(v.memset(bS[:, 132:136], 0.0))
    V(v.memset(wS[:, 0:6], 0.0))
    V(v.memset(wS[:, 138:144], 0.0))
    V(v.memset(msg(9, 10), 0.5))
    fills = V(v.memset(msg(14, 15), 0.5))

    need(2, [LD])
    left = _hand(g, T, topo, core, bS[:, 130:132], helpers, CUT, MW, T.sem.rarr1)
    left += _send(g, T, topo, core, bS[:, 130:132], rank, own, CUT, MW)

    need(1, [LD, fills])
    A(a.activation(b25P[:, 0:136], bS[:], AF.Copy, scale=0.25))
    a2 = A(a.activation(b25S[:], bS[:], AF.Copy, scale=0.25))
    a3 = A(a.activation(junk[:, 0:128], bS[:, 4:132], AF.Square, accum_out=sc[:, 0:1]))
    A(a.activation(msg(22, 24), bS[:, 130:132], AF.Copy))
    need(1, [a3])
    A(a.activation(msg(0, 1), sc[:, 0:1], AF.Copy, scale=0.5))
    need(0, [LD, fills])
    V(v.tensor_tensor(a1P[:, 0:132], bS[:, 1:133], bS[:, 3:135], AL.add))
    need(0, [a2])
    v2 = V(v.tensor_tensor(a2S[:], b25P[:, 0:132], b25S[:, 4:136], AL.add))
    need(0, [v2])
    v3 = V(v.tensor_tensor(wS[:, 6:138], a1P[:, 0:132], a2S[:], AL.add))

    need(1, [v3])
    a5 = A(a.activation(w25P[:, 0:144], wS[:], AF.Copy, scale=0.25))
    A(a.activation(msg(2, 8), wS[:, 132:138], AF.Copy))
    A(a.activation(msg(10, 14), wS[:, 6:10], AF.Copy))
    A(a.activation(junk[:, 144:276], wS[:, 6:138], AF.Square, accum_out=msg(8, 9)))
    need(0, [v3])
    v4 = V(v.tensor_tensor(p1S[:], bS[:, 4:132], wS[:, 8:136], AL.mult))
    need(0, [a5])
    v5 = V(v.tensor_tensor(hwP[:, 0:134], wS[:, 5:139], w25P[:, 6:140], AL.add))
    need(0, [v5])
    v6 = V(v.tensor_tensor(p3S[:], wS[:, 6:138], hwP[:, 2:134], AL.mult))
    v7 = V(v.tensor_tensor(hwmS[:, 0:6], wS[:, 3:9], w25P[:, 2:8], AL.add))
    need(0, [v7])
    v8 = V(v.tensor_tensor(msg(15, 21), hwP[:, 0:6], hwmS[:, 0:6], AL.add))
    need(1, [v4])
    A(a.activation(junk[:, 288:416], p1S[:], AF.Copy, accum_out=msg(21, 22)))
    need(1, [v6])
    a10 = A(a.activation(junk[:, 432:564], p3S[:], AF.Copy, scale=2.0, accum_out=msg(1, 2)))

    need(2, [a10, v8])
    left += _hand(g, T, topo, core, msg(0, CUT), helpers, 0, CUT, T.sem.rarr2)
    left += _send(g, T, topo, core, msg(0, CUT), rank, own, 0, CUT)
    need(1, [v8, a10])
    a11 = A(a.activation(land[:, NR, 9:21], land[:, 0, 9:21], AF.Copy))

    need(0, [ARR, a11])
    g3 = V(v.tensor_tensor(prod[:, 80:150], land[:, 0:NR, 1:8], land[:, 1:NR + 1, 14:21], AL.mult))
    g2 = V(v.tensor_tensor(prod[:, 30:80], land[:, 0:NR, 4:9], land[:, 1:NR + 1, 10:15], AL.mult))
    g1 = V(v.tensor_tensor(prod[:, 0:30], land[:, 0:NR, 21:24], land[:, 1:NR + 1, 9:12], AL.mult))
    V(v.tensor_tensor(wS[:, 8:10], wS[:, 8:10], land[:, NR - 1, 6:8], AL.add))
    h2 = V(v.tensor_tensor(wS[:, 134:136], wS[:, 134:136], land[:, 1, 10:12], AL.add))
    Nc, s1c = sc[:, 4:5], sc[:, 5:6]
    need(1, [ARR, a11])
    r0 = A(a.activation(junk[:, 576:586], land[:, 0:NR, 0], AF.Copy, accum_out=Nc))
    need(1, [r0])
    A(a.activation(sc[:, 8:9], Nc, AF.Copy, scale=3.0))
    A(a.activation(sc[:, 10:11], Nc, AF.Square))
    need(1, [g3])
    A(a.activation(junk[:, 588:658], prod[:, 80:150], AF.Copy, accum_out=sc[:, 7:8]))
    need(1, [g2])
    A(a.activation(junk[:, 660:710], prod[:, 30:80], AF.Copy, accum_out=sc[:, 6:7]))
    need(1, [g1])
    r1 = A(a.activation(junk[:, 0:30], prod[:, 0:30], AF.Copy, accum_out=s1c))
    need(1, [r1])
    dd = A(a.activation(sc[:, 9:10], s1c, AF.Identity, bias=sc[:, 8:9], scale=-1.0))

    Pc, Ec, njc = sc[:, 24:25], sc[:, 25:26], sc[:, 26:27]
    need(0, [r1])
    V(v.tensor_scalar(sc[:, 16:19], sc[:, 5:8], Nc, None, AL.mult))
    t2 = V(v.tensor_scalar(sc[:, 20:22], sc[:, 5:7], s1c, None, AL.mult))
    need(0, [t2])
    t3 = V(v.tensor_tensor(sc[:, 25:27], sc[:, 17:19], sc[:, 20:22], AL.subtract))
    need(0, [t3])
    t4 = V(v.tensor_scalar(Pc, Ec, 3.0, njc, AL.mult, AL.subtract))
    need(1, [t3])
    A(a.activation(sc[:, 11:12], Ec, AF.Copy, scale=s1c))
    e2 = A(a.activation(sc[:, 12:13], Ec, AF.Square))
    need(1, [h2])
    A(a.activation(z2P[:, 0:128], wS[:, 8:136], AF.Copy, scale=Ec))
    need(1, [t4])
    z1 = A(a.activation(T.z1S[:], bS[:, 4:132], AF.Copy, scale=Pc))
    need(0, [t4, e2, dd])
    t5 = V(v.tensor_scalar(sc[:, 13:14], Pc, Nc, sc[:, 11:12], AL.mult, AL.add))
    need(0, [t5])
    t6 = V(v.tensor_scalar(sc[:, 14:15], sc[:, 13:14], sc[:, 9:10], sc[:, 12:13], AL.mult, AL.subtract))
    need(0, [t6])
    V(v.reciprocal(sc[:, 15:16], sc[:, 14:15]))
    need(0, [z1])
    t8 = V(v.tensor_tensor(T.zS[:], T.z1S[:], z2P[:, 0:128], AL.add))
    need(0, [t8])
    t9 = V(v.tensor_scalar(T.yS[:], T.zS[:], sc[:, 15:16], sc[:, 10:11], AL.mult, AL.mult))

    need(3, [t9])
    g.sync.dma_start(T.y[:], T.yS[:]).then_inc(T.sem.st, 16)
    g.sync.wait_ge(T.sem.st, 16)
    g.wait_ge(T.sem.loc, left)
    need(2, [("dv", cnt["dv"]), ("ac", cnt["ac"])])
